import numpy as np
import ml_dtypes


def mxq(x, axis, fmt="e4m3"):
    dtype, down = {"e4m3": (ml_dtypes.float8_e4m3fn, 7), "e5m2": (ml_dtypes.float8_e5m2, 14)}[fmt]
    v = np.moveaxis(np.asarray(x, np.float32).astype(ml_dtypes.bfloat16).astype(np.float64), axis, -1)
    blocks = v.reshape(v.shape[:-1] + (-1, 32))
    amax = np.abs(blocks).max(-1, keepdims=True)
    byte = np.maximum(np.where(amax > 0, np.frexp(amax)[1] - 1 + 127, 0) - down, 1)
    scale = np.exp2(byte - 127.0)
    codes = (blocks / scale).astype(np.float32).astype(dtype).astype(np.float64)
    return np.moveaxis((codes * scale).reshape(v.shape), -1, axis)


WIDE = False


def mx_kscale(k):
    if not WIDE:
        return np.ones(k)
    levels = np.array([10, -10, 5, -5, 0])
    if k % 512:
        return np.exp2(np.random.permutation(np.resize(levels, k // 32))).repeat(32)
    a = np.empty((k // 512, 16))
    for p in range(k // 512):
        a[p, :8] = np.random.permutation(np.resize(levels, 8))
        for g in range(8):
            far = levels[np.abs(levels - a[p, g]) >= 10]
            a[p, g + 8] = far[np.random.randint(len(far))]
    return np.exp2(a.ravel()).repeat(32)


def f64(x):
    return np.asarray(x).astype(np.float64)


def striped(idx):
    return np.tile(idx.reshape(-1, 16).T, (8, 1)).astype(np.uint16)


def unstriped(offs):
    return offs[:16].T.reshape(-1).astype(np.int64)


def striped8(idx):
    return np.concatenate([x.reshape(-1, 16).T for x in idx]).astype(np.uint16)


def runs(offs, k):
    lists = np.stack([offs[16 * r : 16 * r + 16].T.reshape(-1) for r in range(8)]).astype(np.int64)
    return lists[np.arange(k) % 512 // 64]


def pack_weight(w):
    k, n = w.shape
    w = f64(np.asarray(w, np.float32).astype(ml_dtypes.bfloat16)).reshape(k // 32, 32, n)
    amax = np.abs(w).max(1)
    byte = np.clip(np.where(amax > 0, np.frexp(amax)[1] - 1 + 127 - 7, 1), 1, 254)
    scaled = (w * np.exp2(127.0 - byte)[:, None, :]).reshape(k, n).astype(np.float32)
    words = np.ascontiguousarray(scaled.reshape(k // 512, 128, 4, n).transpose(0, 1, 3, 2)).astype(ml_dtypes.float8_e4m3fn).view(np.uint8)
    return words, np.ascontiguousarray(byte.astype(np.uint8).reshape(k // 512, 16, n))


def unpack_weight(words, scales):
    g, p, n, _ = words.shape
    vals = np.ascontiguousarray(words).view(ml_dtypes.float8_e4m3fn).astype(np.float64) * np.repeat(np.exp2(scales.astype(np.float64) - 127.0), 8, axis=1)[..., None]
    return vals.transpose(0, 1, 3, 2).reshape(g * 512, n)


def sigmoid(v):
    return 1.0 / (1.0 + np.exp(-np.maximum(v, -700.0)))


K, T, S, N, H = 512, 2048, 512, 512, 512


def setup_inputs():
    n = np.random.standard_normal
    s = mx_kscale(K)[:, None]
    u = mx_kscale(H)
    packed_xT = pack_weight(n((K, T)) * s)
    return {
        "x_words": packed_xT[0],
        "x_scales": packed_xT[1],
        "w1": (n((K, H)) / np.sqrt(K) / s).astype(np.float32),
        "sl": np.random.uniform(1.0, 2.0, (H, 1)).astype(np.float32),
        "th": (0.5 * n((H, 1))).astype(np.float32),
        "gn": (np.random.uniform(0.5, 1.5, (H, 1)) * u[:, None]).astype(np.float32),
        "w2": (n((H, N)) / np.sqrt(2 * H) / u[:, None]).astype(np.float32),
        "w3": (n((K, N)) / np.sqrt(2 * K) / s).astype(np.float32),
        "offs": striped(np.random.permutation(T)[:S]),
        "n1": striped(np.random.permutation(S)),
        "n2": striped(np.random.permutation(S)),
        "hz": striped8(np.random.randint(0, T, (8, S))),
        "n3": striped8(np.stack([np.random.permutation(S) for _ in range(8)])),
        "n4": striped8(np.stack([np.random.permutation(S) for _ in range(8)])),
        "n5": striped8(np.stack([np.random.permutation(S) for _ in range(8)])),
    }


def reference(x_words, x_scales, w1, sl, th, gn, w2, w3, offs, n1, n2, hz, n3, n4, n5):
    xq = unpack_weight(x_words, x_scales)[:, unstriped(offs)]
    y = mxq(f64(w1), 0, "e4m3").T @ xq
    st = y - y[:, unstriped(n1)]
    sg = sigmoid(f64(sl) * (st[:, unstriped(n2)] - f64(th)))
    z = f64(gn) * (y * sg)
    x_hz = unpack_weight(x_words, x_scales)[np.arange(K)[:, None], runs(hz, K)]
    h = mxq(f64(w2), 0, "e4m3").T @ mxq(z, 0, "e4m3") + mxq(f64(w3), 0, "e4m3").T @ x_hz
    return h + h[np.arange(N)[:, None], runs(n3, N)] - (np.maximum(h[np.arange(N)[:, None], runs(n4, N)], h[np.arange(N)[:, None], runs(n5, N)]))

@@ -1,0 +1,269 @@
+from contextlib import ExitStack
+
+import concourse.mybir as mybir
+
+K, T, S, N, H = 512, 2048, 512, 512, 512
+FLOPS = 3 * 2 * 512 * 512 * 512
+
+F32 = mybir.dt.float32
+BF16 = mybir.dt.bfloat16
+I32 = mybir.dt.int32
+U32 = mybir.dt.uint32
+U16 = mybir.dt.uint16
+U8 = mybir.dt.uint8
+FP8X4 = mybir.dt.float8_e4m3fn_x4
+ALU = mybir.AluOpType
+ACT = mybir.ActivationFunctionType
+
+P = 128
+PACK = 4
+HALF = S // 2
+PAD = 16
+W1_SPLIT = 352
+Z_STEP = 128
+
+
+def tile_picked_mixhehqtrim_none_p_kernel(
+    tc, x_words, x_scales, w1, sl, th, gn, w2, w3, offs, n1, n2, hz, n3, n4, n5, out
+):
+    nc = tc.nc
+    with ExitStack() as ctx:
+        keep = ctx.enter_context(tc.tile_pool(name="keep", bufs=1))
+        psum = ctx.enter_context(tc.psum_pool(name="psum", bufs=1))
+
+        def load_list(name, src):
+            tile = keep.tile([P, S // 16], U16, name=name)
+            nc.sync.dma_start(tile[:], src)
+            return tile
+
+        def entries(lst, c0, c1):
+            return lst[:, c0 // 16 : c1 // 16]
+
+        def load_weight(name, w, c0, c1):
+            raw = keep.tile([P, PACK, c1 - c0], F32, name=name)
+            nc.sync.dma_start(raw[:], w.rearrange("(p j) c -> p j c", j=PACK)[:, :, c0:c1])
+            return raw
+
+        def load_column(name, v):
+            tile = keep.tile([P, PACK], F32, name=name)
+            nc.sync.dma_start(tile[:], v.rearrange("(p t) o -> p (t o)", t=PACK))
+            return tile
+
+        def deal(copy, grouped, raw, raw_c0, c0, c1):
+            dst = grouped[:].rearrange("p (t m j) -> p m j t", t=PACK, j=PACK)[:, c0 // PACK : c1 // PACK]
+            src = raw[:, :, c0 - raw_c0 : c1 - raw_c0].rearrange("p j (m t) -> p m j t", t=PACK)
+            copy(out=dst, in_=src)
+
+        def quantize(codes, scales, src):
+            nc.vector.quantize_mx(out=codes.bitcast(FP8X4), scales=scales, in_=src)
+
+        offs_t = load_list("offs_t", offs)
+        x_bytes = keep.tile([P, T], U8, name="x_bytes", align_bytes=64)
+        for q in range(4):
+            nc.sync.dma_start(
+                x_bytes[32 * q : 32 * q + 32, :].bitcast(I32),
+                x_scales[0, 4 * q : 4 * q + 4, :].bitcast(I32).partition_broadcast(8),
+            )
+        hz_t = load_list("hz_t", hz)
+        x_sb = keep.tile([P, T], I32, name="x_sb", align_bytes=64)
+        nc.sync.dma_start(x_sb[:], x_words[0].rearrange("p n t -> p (n t)").bitcast(I32))
+        w1_raw = [load_weight(f"w1_raw{u}", w1, u * HALF, (u + 1) * HALF) for u in range(2)]
+        n1_t = load_list("n1_t", n1)
+        sl_t = load_column("sl_t", sl)
+        th_t = load_column("th_t", th)
+        w3_raw = load_weight("w3_raw", w3, 0, N)
+        w2_raw = load_weight("w2_raw", w2, 0, N)
+        n2_t = load_list("n2_t", n2)
+        gn_t = load_column("gn_t", gn)
+        n4_t = load_list("n4_t", n4)
+        n5_t = load_list("n5_t", n5)
+        n3_t = load_list("n3_t", n3)
+
+        xo_scales = keep.tile([P, S], U8, name="xo_scales", align_bytes=64)
+        xo_words = keep.tile([P, S], U32, name="xo_words", align_bytes=64)
+        nc.vector.tensor_copy(xo_scales[:], x_bytes[:].indirect(offs_t[:]))
+        nc.vector.tensor_copy(xo_words[:], x_sb[:].bitcast(U32).indirect(offs_t[:]))
+
+        w1_g = keep.tile([P, PACK * H], BF16, name="w1_g", tag="w1_stage", align_bytes=64)
+        w1_codes = keep.tile([P, H], U32, name="w1_codes", align_bytes=64)
+        w1_scales = keep.tile([P, H], U8, name="w1_scales", align_bytes=64)
+        deal(nc.scalar.copy, w1_g, w1_raw[0], 0, 0, HALF)
+        deal(nc.scalar.copy, w1_g, w1_raw[1], HALF, HALF, W1_SPLIT)
+        deal(nc.vector.tensor_copy, w1_g, w1_raw[1], HALF, W1_SPLIT, H)
+
+        def pair_banks(name):
+            return [[psum.tile([P, 2, HALF], F32, name=f"{name}{u}{b}") for b in range(2)] for u in range(2)]
+
+        def in_bank(banks, t, c0, c1):
+            u = c0 // HALF
+            return banks[u][(t + 1) // 2 % 2][:, t // 2, c0 - u * HALF : c1 - u * HALF]
+
+        y_ps = pair_banks("y_ps")
+        y_sb = [keep.tile([P, S + PAD], F32, name=f"y_sb{t}") for t in range(PACK)]
+        for t in range(PACK):
+            nc.gpsimd.memset(y_sb[t][:, S:], 0.0)
+        for t in range(PACK):
+            cols = slice(t * P, (t + 1) * P)
+            quantize(w1_codes[:, cols], w1_scales[:, cols], w1_g[:, t * H : (t + 1) * H])
+        for t in range(PACK):
+            cols = slice(t * P, (t + 1) * P)
+            for c0 in (0, HALF):
+                c1 = c0 + HALF
+                nc.tensor.matmul_mx(
+                    out=in_bank(y_ps, t, c0, c1),
+                    lhsT=w1_codes[:, cols].bitcast(FP8X4),
+                    lhsT_scale=w1_scales[:, cols],
+                    rhs=xo_words[:, c0:c1].bitcast(FP8X4),
+                    rhs_scale=xo_scales[:, c0:c1],
+                    start=True,
+                    stop=True,
+                )
+                if t == 0:
+                    nc.scalar.copy(out=y_sb[t][:, c0:c1], in_=in_bank(y_ps, t, c0, c1))
+                else:
+                    nc.vector.tensor_copy(out=y_sb[t][:, c0:c1], in_=in_bank(y_ps, t, c0, c1))
+
+        xh_picked = keep.tile([P, S], U8, name="xh_picked", align_bytes=64)
+        xh_words = [
+            keep.tile([P, HALF], U32, name="xh_words0", align_bytes=64),
+            keep.tile([P, HALF], U32, name="xh_words1", tag="w1_stage", align_bytes=64),
+        ]
+        xh_scales = keep.tile([P, S], U8, name="xh_scales", align_bytes=64)
+        nc.vector.tensor_copy(xh_picked[:], x_bytes[:].indirect(hz_t[:]))
+        nc.vector.tensor_copy(xh_scales[:].bitcast(I32), xh_picked[:].bitcast(I32))
+        for u in range(2):
+            nc.vector.tensor_copy(
+                xh_words[u][:], x_sb[:].bitcast(U32).indirect(entries(hz_t, u * HALF, (u + 1) * HALF))
+            )
+        for r in (2, 3):
+            nc.sync.dma_start(xh_scales[r:P:32, :].bitcast(I32), xh_picked[16 + r : P : 32, :].bitcast(I32))
+
+        bias_t = keep.tile([P, PACK], F32, name="bias_t")
+        nc.vector.scalar_tensor_tensor(bias_t[:], th_t[:], -1.0, sl_t[:], ALU.mult, ALU.mult)
+
+        h_sb = [keep.tile([P, S], F32, name=f"h_sb{t}") for t in range(PACK)]
+        y_n1 = []
+        for t in range(PACK - 1):
+            whole = keep.tile([P, S], F32, name=f"y_n1_{t}", tag=f"y_n1_{t}", align_bytes=64)
+            nc.scalar.activation(whole[:], y_sb[t][:].indirect(n1_t[:]), ACT.Copy)
+            y_n1.append([whole[:, :HALF], whole[:, HALF:]])
+        halves = []
+        for u in range(2):
+            part = keep.tile([P, HALF], F32, name=f"y_n1_last{u}", tag=f"y_n1_last{u}", align_bytes=64)
+            nc.scalar.activation(part[:], y_sb[PACK - 1][:].indirect(entries(n1_t, u * HALF, (u + 1) * HALF)), ACT.Copy)
+            halves.append(part[:])
+        y_n1.append(halves)
+
+        def quantize_weight(name, raw, codes_tag):
+            g = keep.tile([P, PACK * N], BF16, name=f"{name}_g", tag=f"{name}_stage", align_bytes=64)
+            codes = keep.tile([P, N], U32, name=f"{name}_codes", tag=codes_tag, align_bytes=64)
+            scales = keep.tile([P, N], U8, name=f"{name}_scales", align_bytes=64)
+            for t in range(PACK):
+                nc.gpsimd.tensor_scalar(
+                    g[:, t * N : (t + 1) * N].rearrange("p (b i j) -> p b i j", i=8, j=PACK),
+                    raw[:].rearrange("p j (b t i) -> p t b i j", t=PACK, i=8)[:, t],
+                    1.0,
+                    0.0,
+                    ALU.mult,
+                    ALU.add,
+                )
+            quantize(codes[:], scales[:], g[:])
+            return codes, scales
+
+        def difference(t):
+            st_t = keep.tile([P, S], F32, name=f"st{t}")
+            for c0 in (0, HALF):
+                c1 = c0 + HALF
+                nc.vector.tensor_tensor(st_t[:, c0:c1], in_bank(y_ps, t, c0, c1), y_n1[t][c0 // HALF], ALU.subtract)
+            return st_t
+
+        st = [difference(t) for t in range(PACK)]
+        w3_codes, w3_scales = quantize_weight("w3", w3_raw, "y_n1_1")
+        w2_codes, w2_scales = quantize_weight("w2", w2_raw, "y_n1_last0")
+
+        z_codes = keep.tile([P, S], U32, name="z_codes", align_bytes=64)
+        z_scales = keep.tile([P, S], U8, name="z_scales", align_bytes=64)
+        z_all = keep.tile([P, PACK * S], BF16, name="z_all", tag="w2_stage", align_bytes=64)
+        sg_early = keep.tile([P, PACK * Z_STEP], F32, name="sg_early")
+        sg_late = keep.tile([P, PACK * (S - Z_STEP)], F32, name="sg_late", tag="y_n1_last1", align_bytes=64)
+        h_ps = pair_banks("h_ps")
+
+        def h_bank(t, c0, c1):
+            return in_bank(h_ps, t, c0, c1)
+
+        for c0 in (0, HALF):
+            for t in range(PACK):
+                cols = slice(t * P, (t + 1) * P)
+                nc.tensor.matmul_mx(
+                    out=h_bank(t, c0, c0 + HALF),
+                    lhsT=w3_codes[:, cols].bitcast(FP8X4),
+                    lhsT_scale=w3_scales[:, cols],
+                    rhs=xh_words[c0 // HALF][:].bitcast(FP8X4),
+                    rhs_scale=xh_scales[:, c0 : c0 + HALF],
+                    start=(t < 2),
+                    stop=False,
+                )
+
+        for c0 in range(0, S, Z_STEP):
+            c1 = c0 + Z_STEP
+            width = c1 - c0
+            z_rows = z_all[:, PACK * c0 : PACK * c1].rearrange("p (t c) -> p t c", t=PACK)
+            z_g = keep.tile([P, width * PACK], BF16, name=f"z_g{c0}", align_bytes=64)
+            for t in range(PACK):
+                first = PACK * max(c0 - Z_STEP, 0) + t * width
+                sg = (sg_early if c0 == 0 else sg_late)[:, first : first + width]
+                nc.scalar.activation(
+                    sg,
+                    st[t][:].indirect(entries(n2_t, c0, c1)),
+                    ACT.Sigmoid,
+                    bias=bias_t[:, t : t + 1],
+                    scale=sl_t[:, t : t + 1],
+                )
+                nc.vector.scalar_tensor_tensor(
+                    z_rows[:, t, :], in_bank(y_ps, t, c0, c1), gn_t[:, t : t + 1], sg, ALU.mult, ALU.mult
+                )
+            nc.vector.tensor_copy(
+                out=z_g[:].rearrange("p (c i t) -> p c t i", i=4, t=PACK),
+                in_=z_rows.rearrange("p t (c i) -> p c t i", i=4),
+            )
+            quantize(z_codes[:, c0:c1], z_scales[:, c0:c1], z_g[:])
+            for t in (3, 0, 2, 1):
+                cols = slice(t * P, (t + 1) * P)
+                nc.tensor.matmul_mx(
+                    out=h_bank(t, c0, c1),
+                    lhsT=w2_codes[:, cols].bitcast(FP8X4),
+                    lhsT_scale=w2_scales[:, cols],
+                    rhs=z_codes[:, c0:c1].bitcast(FP8X4),
+                    rhs_scale=z_scales[:, c0:c1],
+                    start=False,
+                    stop=(t < 2 and c1 % HALF == 0),
+                )
+        nc.scalar.copy(out=h_sb[0][:, HALF:S], in_=h_bank(0, HALF, S))
+        for t in range(1, PACK):
+            nc.vector.tensor_copy(out=h_sb[t][:, HALF:S], in_=h_bank(t, HALF, S))
+        for t in range(PACK):
+            nc.scalar.copy(out=h_sb[t][:, 0:HALF], in_=h_bank(t, 0, HALF))
+
+        out_rows = out.rearrange("(b t i) s -> t b i s", t=PACK, i=8)
+        steps = [(t, c0, c0 + HALF) for t in range(PACK) for c0 in (0, HALF)][:-1] + [(3, 256, 384), (3, 384, 512)]
+        rests = []
+
+        def finish(n):
+            t, c0, c1 = steps[n]
+            res = keep.tile([P, c1 - c0], F32, name=f"res_{n}")
+            nc.vector.tensor_tensor(res[:], h_sb[t][:].indirect(entries(n3_t, c0, c1)), rests[n][:], ALU.add)
+            nc.sync.dma_start(out_rows[t][:, :, c0:c1], res[:])
+
+        for n, (t, c0, c1) in enumerate(steps):
+            h4 = keep.tile([P, c1 - c0], F32, name=f"h4_{n}")
+            h5 = keep.tile([P, c1 - c0], F32, name=f"h5_{n}")
+            top = keep.tile([P, c1 - c0], F32, name=f"top_{n}")
+            rest = keep.tile([P, c1 - c0], F32, name=f"rest_{n}")
+            rests.append(rest)
+            nc.scalar.activation(h4[:], h_sb[t][:].indirect(entries(n4_t, c0, c1)), ACT.Copy)
+            nc.scalar.activation(h5[:], h_sb[t][:].indirect(entries(n5_t, c0, c1)), ACT.Copy)
+            nc.vector.tensor_tensor(top[:], h4[:], h5[:], ALU.max)
+            if n > 0:
+                finish(n - 1)
+            nc.vector.tensor_tensor(rest[:], h_sb[t][:, c0:c1], top[:], ALU.subtract)
+        finish(len(steps) - 1)

@@ -79,6 +79,10 @@ def tile_picked_mixhehqtrim_none_p_kernel(
         n5_t = load_list("n5_t", n5)
         n3_t = load_list("n3_t", n3)
 
+        warm = keep.tile([P, 8], F32, name="warm")
+        warm2 = keep.tile([P, 8], F32, name="warm2")
+        nc.vector.memset(warm[:], 0.0)
+        nc.scalar.activation(warm2[:], warm[:], ACT.Sigmoid)
         xo_scales = keep.tile([P, S], U8, name="xo_scales", align_bytes=64)
         xo_words = keep.tile([P, S], U32, name="xo_words", align_bytes=64)
         nc.vector.tensor_copy(xo_scales[:], x_bytes[:].indirect(offs_t[:]))

@@ -50,8 +50,8 @@ def tile_picked_mixhehqtrim_none_p_kernel(
             return tile
 
         def deal(copy, grouped, raw, raw_c0, c0, c1):
-            dst = grouped[:].rearrange("p (t m j) -> p m j t", t=PACK, j=PACK)[:, c0 // PACK : c1 // PACK]
-            src = raw[:, :, c0 - raw_c0 : c1 - raw_c0].rearrange("p j (m t) -> p m j t", t=PACK)
+            dst = grouped[:].rearrange("p (t m j) -> p m t j", t=PACK, j=PACK)[:, c0 // PACK : c1 // PACK]
+            src = raw[:, :, c0 - raw_c0 : c1 - raw_c0].rearrange("p j (m t) -> p m t j", t=PACK)
             copy(out=dst, in_=src)
 
         def quantize(codes, scales, src):
@@ -122,10 +122,8 @@ def tile_picked_mixhehqtrim_none_p_kernel(
                     start=True,
                     stop=True,
                 )
-                if t == 0:
-                    nc.scalar.copy(out=y_sb[t][:, c0:c1], in_=in_bank(y_ps, t, c0, c1))
-                else:
-                    nc.vector.tensor_copy(out=y_sb[t][:, c0:c1], in_=in_bank(y_ps, t, c0, c1))
+                copy = nc.vector.tensor_copy if t == PACK - 1 else nc.scalar.copy
+                copy(out=y_sb[t][:, c0:c1], in_=in_bank(y_ps, t, c0, c1))
 
         xh_picked = keep.tile([P, S], U8, name="xh_picked", align_bytes=64)
         xh_words = [
@@ -146,50 +144,42 @@ def tile_picked_mixhehqtrim_none_p_kernel(
         nc.vector.scalar_tensor_tensor(bias_t[:], th_t[:], -1.0, sl_t[:], ALU.mult, ALU.mult)
 
         h_sb = [keep.tile([P, S], F32, name=f"h_sb{t}") for t in range(PACK)]
-        y_n1 = []
-        for t in range(PACK - 1):
-            whole = keep.tile([P, S], F32, name=f"y_n1_{t}", tag=f"y_n1_{t}", align_bytes=64)
-            nc.scalar.activation(whole[:], y_sb[t][:].indirect(n1_t[:]), ACT.Copy)
-            y_n1.append([whole[:, :HALF], whole[:, HALF:]])
-        halves = []
-        for u in range(2):
-            part = keep.tile([P, HALF], F32, name=f"y_n1_last{u}", tag=f"y_n1_last{u}", align_bytes=64)
-            nc.scalar.activation(part[:], y_sb[PACK - 1][:].indirect(entries(n1_t, u * HALF, (u + 1) * HALF)), ACT.Copy)
-            halves.append(part[:])
-        y_n1.append(halves)
+        y_n1 = [keep.tile([P, S], F32, name=f"y_n1_{t}", tag=f"y_n1_{t}") for t in range(PACK)]
+        for t in range(PACK):
+            nc.scalar.activation(y_n1[t][:], y_sb[t][:].indirect(n1_t[:]), ACT.Copy)
 
-        def quantize_weight(name, raw, codes_tag):
-            g = keep.tile([P, PACK * N], BF16, name=f"{name}_g", tag=f"{name}_stage", align_bytes=64)
-            codes = keep.tile([P, N], U32, name=f"{name}_codes", tag=codes_tag, align_bytes=64)
+        def quantize_weight(name, raw):
+            codes = keep.tile([P, N], U32, name=f"{name}_codes", align_bytes=64)
             scales = keep.tile([P, N], U8, name=f"{name}_scales", align_bytes=64)
+            staged = []
             for t in range(PACK):
-                nc.gpsimd.tensor_scalar(
-                    g[:, t * N : (t + 1) * N].rearrange("p (b i j) -> p b i j", i=8, j=PACK),
-                    raw[:].rearrange("p j (b t i) -> p t b i j", t=PACK, i=8)[:, t],
-                    1.0,
-                    0.0,
-                    ALU.mult,
-                    ALU.add,
+                g = keep.tile([P, PACK * P], BF16, name=f"{name}_g{t}", tag=f"{name}_stage{t}", align_bytes=64)
+                nc.vector.tensor_copy(
+                    out=g[:].rearrange("p (b q i j) -> p b q j i", q=2, i=4, j=PACK),
+                    in_=raw[:].rearrange("p j (b t q i) -> p t b q j i", t=PACK, q=2, i=4)[:, t],
                 )
-            quantize(codes[:], scales[:], g[:])
+                staged.append(g)
+            for t in range(PACK):
+                cols = slice(t * P, (t + 1) * P)
+                quantize(codes[:, cols], scales[:, cols], staged[t][:])
             return codes, scales
 
         def difference(t):
-            st_t = keep.tile([P, S], F32, name=f"st{t}")
+            st_t = keep.tile([P, S], F32, name=f"st{t}", tag=f"w2_stage{t}", align_bytes=64)
             for c0 in (0, HALF):
                 c1 = c0 + HALF
-                nc.vector.tensor_tensor(st_t[:, c0:c1], in_bank(y_ps, t, c0, c1), y_n1[t][c0 // HALF], ALU.subtract)
+                nc.vector.tensor_tensor(st_t[:, c0:c1], in_bank(y_ps, t, c0, c1), y_n1[t][:, c0:c1], ALU.subtract)
             return st_t
 
+        w3_codes, w3_scales = quantize_weight("w3", w3_raw)
+        w2_codes, w2_scales = quantize_weight("w2", w2_raw)
         st = [difference(t) for t in range(PACK)]
-        w3_codes, w3_scales = quantize_weight("w3", w3_raw, "y_n1_1")
-        w2_codes, w2_scales = quantize_weight("w2", w2_raw, "y_n1_last0")
 
         z_codes = keep.tile([P, S], U32, name="z_codes", align_bytes=64)
         z_scales = keep.tile([P, S], U8, name="z_scales", align_bytes=64)
-        z_all = keep.tile([P, PACK * S], BF16, name="z_all", tag="w2_stage", align_bytes=64)
+        z_all = keep.tile([P, PACK * S], BF16, name="z_all")
         sg_early = keep.tile([P, PACK * Z_STEP], F32, name="sg_early")
-        sg_late = keep.tile([P, PACK * (S - Z_STEP)], F32, name="sg_late", tag="y_n1_last1", align_bytes=64)
+        sg_late = keep.tile([P, PACK * (S - Z_STEP)], F32, name="sg_late", tag=f"y_n1_{PACK - 1}")
         h_ps = pair_banks("h_ps")
 
         def h_bank(t, c0, c1):

@@ -58,16 +58,20 @@ def tile_picked_mixhehqtrim_none_p_kernel(
             nc.vector.quantize_mx(out=codes.bitcast(FP8X4), scales=scales, in_=src)
 
         offs_t = load_list("offs_t", offs)
-        x_bytes = keep.tile([P, T], U8, name="x_bytes", align_bytes=64)
+        hz_t = load_list("hz_t", hz)
+        w1_raw = [load_weight("w1_raw0", w1, 0, HALF)]
+        xo_bytes = keep.tile([P, T], U8, name="xo_bytes", align_bytes=64)
+        nc.vector.memset(xo_bytes[:].bitcast(I32), 0)
         for q in range(4):
             nc.sync.dma_start(
-                x_bytes[32 * q : 32 * q + 32, :].bitcast(I32),
-                x_scales[0, 4 * q : 4 * q + 4, :].bitcast(I32).partition_broadcast(8),
+                xo_bytes[32 * q : 32 * q + 4, :].bitcast(I32), x_scales[0, 4 * q : 4 * q + 4, :].bitcast(I32)
             )
-        hz_t = load_list("hz_t", hz)
+        xh_bytes = keep.tile([P, T], U8, name="xh_bytes", align_bytes=64)
+        nc.vector.memset(xh_bytes[:].bitcast(I32), 0)
+        nc.sync.dma_start(xh_bytes[0:P:8, :].bitcast(I32), x_scales[0].bitcast(I32))
         x_sb = keep.tile([P, T], I32, name="x_sb", align_bytes=64)
         nc.sync.dma_start(x_sb[:], x_words[0].rearrange("p n t -> p (n t)").bitcast(I32))
-        w1_raw = [load_weight(f"w1_raw{u}", w1, u * HALF, (u + 1) * HALF) for u in range(2)]
+        w1_raw.append(load_weight("w1_raw1", w1, HALF, H))
         n1_t = load_list("n1_t", n1)
         sl_t = load_column("sl_t", sl)
         th_t = load_column("th_t", th)
@@ -85,7 +89,7 @@ def tile_picked_mixhehqtrim_none_p_kernel(
         nc.scalar.activation(warm2[:], warm[:], ACT.Sigmoid)
         xo_scales = keep.tile([P, S], U8, name="xo_scales", align_bytes=64)
         xo_words = keep.tile([P, S], U32, name="xo_words", align_bytes=64)
-        nc.vector.tensor_copy(xo_scales[:], x_bytes[:].indirect(offs_t[:]))
+        nc.vector.tensor_copy(xo_scales[:], xo_bytes[:].indirect(offs_t[:]))
         nc.vector.tensor_copy(xo_words[:], x_sb[:].bitcast(U32).indirect(offs_t[:]))
 
         w1_g = keep.tile([P, PACK * H], BF16, name="w1_g", tag="w1_stage", align_bytes=64)
@@ -105,7 +109,7 @@ def tile_picked_mixhehqtrim_none_p_kernel(
         y_ps = pair_banks("y_ps")
         y_sb = [keep.tile([P, S + PAD], F32, name=f"y_sb{t}") for t in range(PACK)]
         for t in range(PACK):
-            nc.gpsimd.memset(y_sb[t][:, S:], 0.0)
+            nc.vector.memset(y_sb[t][:, S:], 0.0)
         for t in range(PACK):
             cols = slice(t * P, (t + 1) * P)
             quantize(w1_codes[:, cols], w1_scales[:, cols], w1_g[:, t * H : (t + 1) * H])
@@ -126,19 +130,13 @@ def tile_picked_mixhehqtrim_none_p_kernel(
                 copy(out=y_sb[t][:, c0:c1], in_=in_bank(y_ps, t, c0, c1))
 
         xh_picked = keep.tile([P, S], U8, name="xh_picked", align_bytes=64)
-        xh_words = [
-            keep.tile([P, HALF], U32, name="xh_words0", align_bytes=64),
-            keep.tile([P, HALF], U32, name="xh_words1", tag="w1_stage", align_bytes=64),
-        ]
+        xh_words = keep.tile([P, S], U32, name="xh_words", tag="w1_stage", align_bytes=64)
         xh_scales = keep.tile([P, S], U8, name="xh_scales", align_bytes=64)
-        nc.vector.tensor_copy(xh_picked[:], x_bytes[:].indirect(hz_t[:]))
+        nc.vector.tensor_copy(xh_picked[:], xh_bytes[:].indirect(hz_t[:]))
         nc.vector.tensor_copy(xh_scales[:].bitcast(I32), xh_picked[:].bitcast(I32))
-        for u in range(2):
-            nc.vector.tensor_copy(
-                xh_words[u][:], x_sb[:].bitcast(U32).indirect(entries(hz_t, u * HALF, (u + 1) * HALF))
-            )
-        for r in (2, 3):
-            nc.sync.dma_start(xh_scales[r:P:32, :].bitcast(I32), xh_picked[16 + r : P : 32, :].bitcast(I32))
+        nc.vector.tensor_copy(xh_words[:], x_sb[:].bitcast(U32).indirect(hz_t[:]))
+        for r in (1, 2, 3):
+            nc.sync.dma_start(xh_scales[r:P:32, :].bitcast(I32), xh_picked[8 * r : P : 32, :].bitcast(I32))
 
         bias_t = keep.tile([P, PACK], F32, name="bias_t")
         nc.vector.scalar_tensor_tensor(bias_t[:], th_t[:], -1.0, sl_t[:], ALU.mult, ALU.mult)
@@ -192,7 +190,7 @@ def tile_picked_mixhehqtrim_none_p_kernel(
                     out=h_bank(t, c0, c0 + HALF),
                     lhsT=w3_codes[:, cols].bitcast(FP8X4),
                     lhsT_scale=w3_scales[:, cols],
-                    rhs=xh_words[c0 // HALF][:].bitcast(FP8X4),
+                    rhs=xh_words[:, c0 : c0 + HALF].bitcast(FP8X4),
                     rhs_scale=xh_scales[:, c0 : c0 + HALF],
                     start=(t < 2),
                     stop=False,

@@ -2,7 +2,7 @@ from contextlib import ExitStack
 
 import concourse.mybir as mybir
 
-K, T, S, N, H = 512, 2048, 512, 512, 512
+T, S, N, H = 2048, 512, 512, 512
 FLOPS = 3 * 2 * 512 * 512 * 512
 
 F32 = mybir.dt.float32
@@ -17,10 +17,12 @@ ACT = mybir.ActivationFunctionType
 
 P = 128
 PACK = 4
+LAST = PACK - 1
 HALF = S // 2
+STRETCH = 128
+LAST_C0 = S - STRETCH
 PAD = 16
 W1_SPLIT = 352
-Z_STEP = 128
 
 
 def tile_picked_mixhehqtrim_none_p_kernel(
@@ -44,22 +46,29 @@ def tile_picked_mixhehqtrim_none_p_kernel(
             nc.sync.dma_start(raw[:], w.rearrange("(p j) c -> p j c", j=PACK)[:, :, c0:c1])
             return raw
 
-        def load_column(name, v):
+        def load_rows(name, v):
             tile = keep.tile([P, PACK], F32, name=name)
             nc.sync.dma_start(tile[:], v.rearrange("(p t) o -> p (t o)", t=PACK))
             return tile
 
-        def deal(copy, grouped, raw, raw_c0, c0, c1):
-            dst = grouped[:].rearrange("p (t m j) -> p m t j", t=PACK, j=PACK)[:, c0 // PACK : c1 // PACK]
-            src = raw[:, :, c0 - raw_c0 : c1 - raw_c0].rearrange("p j (m t) -> p m t j", t=PACK)
-            copy(out=dst, in_=src)
-
         def quantize(codes, scales, src):
             nc.vector.quantize_mx(out=codes.bitcast(FP8X4), scales=scales, in_=src)
 
+        def product(acc, w_codes, w_scales, t, codes, scales, c0, c1, start, stop):
+            cols = slice(t * P, (t + 1) * P)
+            nc.tensor.matmul_mx(
+                out=acc,
+                lhsT=w_codes[:, cols].bitcast(FP8X4),
+                lhsT_scale=w_scales[:, cols],
+                rhs=codes[:, c0:c1].bitcast(FP8X4),
+                rhs_scale=scales[:, c0:c1],
+                start=start,
+                stop=stop,
+            )
+
         offs_t = load_list("offs_t", offs)
         hz_t = load_list("hz_t", hz)
-        w1_raw = [load_weight("w1_raw0", w1, 0, HALF)]
+        w1_raw0 = load_weight("w1_raw0", w1, 0, HALF)
         xo_bytes = keep.tile([P, T], U8, name="xo_bytes", align_bytes=64)
         nc.vector.memset(xo_bytes[:].bitcast(I32), 0)
         for q in range(4):
@@ -70,64 +79,63 @@ def tile_picked_mixhehqtrim_none_p_kernel(
         nc.vector.memset(xh_bytes[:].bitcast(I32), 0)
         nc.sync.dma_start(xh_bytes[0:P:8, :].bitcast(I32), x_scales[0].bitcast(I32))
         x_sb = keep.tile([P, T], I32, name="x_sb", align_bytes=64)
-        nc.sync.dma_start(x_sb[:], x_words[0].rearrange("p n t -> p (n t)").bitcast(I32))
-        w1_raw.append(load_weight("w1_raw1", w1, HALF, H))
+        nc.sync.dma_start(x_sb[:], x_words[0].rearrange("p n j -> p (n j)").bitcast(I32))
+        w1_raw1 = load_weight("w1_raw1", w1, HALF, H)
         n1_t = load_list("n1_t", n1)
-        sl_t = load_column("sl_t", sl)
-        th_t = load_column("th_t", th)
+        sl_t = load_rows("sl_t", sl)
+        th_t = load_rows("th_t", th)
         w3_raw = load_weight("w3_raw", w3, 0, N)
         w2_raw = load_weight("w2_raw", w2, 0, N)
         n2_t = load_list("n2_t", n2)
-        gn_t = load_column("gn_t", gn)
+        gn_t = load_rows("gn_t", gn)
         n4_t = load_list("n4_t", n4)
         n5_t = load_list("n5_t", n5)
         n3_t = load_list("n3_t", n3)
 
-        warm = keep.tile([P, 8], F32, name="warm")
-        warm2 = keep.tile([P, 8], F32, name="warm2")
-        nc.vector.memset(warm[:], 0.0)
-        nc.scalar.activation(warm2[:], warm[:], ACT.Sigmoid)
+        warm_in = keep.tile([P, 8], F32, name="warm_in")
+        warm_out = keep.tile([P, 8], F32, name="warm_out")
+        nc.vector.memset(warm_in[:], 0.0)
+        nc.scalar.activation(warm_out[:], warm_in[:], ACT.Sigmoid)
+
         xo_scales = keep.tile([P, S], U8, name="xo_scales", align_bytes=64)
         xo_words = keep.tile([P, S], U32, name="xo_words", align_bytes=64)
         nc.vector.tensor_copy(xo_scales[:], xo_bytes[:].indirect(offs_t[:]))
         nc.vector.tensor_copy(xo_words[:], x_sb[:].bitcast(U32).indirect(offs_t[:]))
 
-        w1_g = keep.tile([P, PACK * H], BF16, name="w1_g", tag="w1_stage", align_bytes=64)
+        w1_bf = keep.tile([P, PACK * H], BF16, name="w1_bf", tag="w1_stage", align_bytes=64)
         w1_codes = keep.tile([P, H], U32, name="w1_codes", align_bytes=64)
         w1_scales = keep.tile([P, H], U8, name="w1_scales", align_bytes=64)
-        deal(nc.scalar.copy, w1_g, w1_raw[0], 0, 0, HALF)
-        deal(nc.scalar.copy, w1_g, w1_raw[1], HALF, HALF, W1_SPLIT)
-        deal(nc.vector.tensor_copy, w1_g, w1_raw[1], HALF, W1_SPLIT, H)
 
-        def pair_banks(name):
-            return [[psum.tile([P, 2, HALF], F32, name=f"{name}{u}{b}") for b in range(2)] for u in range(2)]
+        def round_w1(copy, raw, raw_c0, c0, c1):
+            copy(
+                out=w1_bf[:].rearrange("p (t m j) -> p m t j", t=PACK, j=PACK)[:, c0 // PACK : c1 // PACK],
+                in_=raw[:, :, c0 - raw_c0 : c1 - raw_c0].rearrange("p j (m t) -> p m t j", t=PACK),
+            )
 
-        def in_bank(banks, t, c0, c1):
+        round_w1(nc.scalar.copy, w1_raw0, 0, 0, HALF)
+        round_w1(nc.scalar.copy, w1_raw1, HALF, HALF, W1_SPLIT)
+        round_w1(nc.vector.tensor_copy, w1_raw1, HALF, W1_SPLIT, H)
+
+        y_ps = [
+            [psum.tile([P, 2, HALF], F32, name=f"y_ps{u}{b}", tag=f"y_ps{u}{b}") for b in range(2)] for u in range(2)
+        ]
+
+        def y_acc(t, c0, c1):
             u = c0 // HALF
-            return banks[u][(t + 1) // 2 % 2][:, t // 2, c0 - u * HALF : c1 - u * HALF]
+            return y_ps[u][(t + 1) // 2 % 2][:, t // 2, c0 - u * HALF : c1 - u * HALF]
 
-        y_ps = pair_banks("y_ps")
         y_sb = [keep.tile([P, S + PAD], F32, name=f"y_sb{t}") for t in range(PACK)]
         for t in range(PACK):
             nc.vector.memset(y_sb[t][:, S:], 0.0)
         for t in range(PACK):
             cols = slice(t * P, (t + 1) * P)
-            quantize(w1_codes[:, cols], w1_scales[:, cols], w1_g[:, t * H : (t + 1) * H])
+            quantize(w1_codes[:, cols], w1_scales[:, cols], w1_bf[:, t * H : (t + 1) * H])
         for t in range(PACK):
-            cols = slice(t * P, (t + 1) * P)
+            copy = nc.vector.tensor_copy if t == LAST else nc.scalar.copy
             for c0 in (0, HALF):
                 c1 = c0 + HALF
-                nc.tensor.matmul_mx(
-                    out=in_bank(y_ps, t, c0, c1),
-                    lhsT=w1_codes[:, cols].bitcast(FP8X4),
-                    lhsT_scale=w1_scales[:, cols],
-                    rhs=xo_words[:, c0:c1].bitcast(FP8X4),
-                    rhs_scale=xo_scales[:, c0:c1],
-                    start=True,
-                    stop=True,
-                )
-                copy = nc.vector.tensor_copy if t == PACK - 1 else nc.scalar.copy
-                copy(out=y_sb[t][:, c0:c1], in_=in_bank(y_ps, t, c0, c1))
+                product(y_acc(t, c0, c1), w1_codes, w1_scales, t, xo_words, xo_scales, c0, c1, True, True)
+                copy(out=y_sb[t][:, c0:c1], in_=y_acc(t, c0, c1))
 
         xh_picked = keep.tile([P, S], U8, name="xh_picked", align_bytes=64)
         xh_words = keep.tile([P, S], U32, name="xh_words", tag="w1_stage", align_bytes=64)
@@ -149,61 +157,66 @@ def tile_picked_mixhehqtrim_none_p_kernel(
         def quantize_weight(name, raw):
             codes = keep.tile([P, N], U32, name=f"{name}_codes", align_bytes=64)
             scales = keep.tile([P, N], U8, name=f"{name}_scales", align_bytes=64)
-            staged = []
+            rounded = []
             for t in range(PACK):
-                g = keep.tile([P, PACK * P], BF16, name=f"{name}_g{t}", tag=f"{name}_stage{t}", align_bytes=64)
+                bf = keep.tile([P, PACK * P], BF16, name=f"{name}_bf{t}", tag=f"{name}_stage{t}", align_bytes=64)
                 nc.vector.tensor_copy(
-                    out=g[:].rearrange("p (b q i j) -> p b q j i", q=2, i=4, j=PACK),
-                    in_=raw[:].rearrange("p j (b t q i) -> p t b q j i", t=PACK, q=2, i=4)[:, t],
+                    out=bf[:].rearrange("p (b q e j) -> p b q j e", q=2, e=4, j=PACK),
+                    in_=raw[:].rearrange("p j (b t q e) -> p t b q j e", t=PACK, q=2, e=4)[:, t],
                 )
-                staged.append(g)
+                rounded.append(bf)
             for t in range(PACK):
                 cols = slice(t * P, (t + 1) * P)
-                quantize(codes[:, cols], scales[:, cols], staged[t][:])
+                quantize(codes[:, cols], scales[:, cols], rounded[t][:])
             return codes, scales
-
-        def difference(t):
-            st_t = keep.tile([P, S], F32, name=f"st{t}", tag=f"w2_stage{t}", align_bytes=64)
-            for c0 in (0, HALF):
-                c1 = c0 + HALF
-                nc.vector.tensor_tensor(st_t[:, c0:c1], in_bank(y_ps, t, c0, c1), y_n1[t][:, c0:c1], ALU.subtract)
-            return st_t
 
         w3_codes, w3_scales = quantize_weight("w3", w3_raw)
         w2_codes, w2_scales = quantize_weight("w2", w2_raw)
-        st = [difference(t) for t in range(PACK)]
+
+        st = []
+        for t in range(PACK):
+            st_t = keep.tile([P, S], F32, name=f"st{t}", tag=f"w2_stage{t}", align_bytes=64)
+            for c0 in (0, HALF):
+                c1 = c0 + HALF
+                nc.vector.tensor_tensor(st_t[:, c0:c1], y_acc(t, c0, c1), y_n1[t][:, c0:c1], ALU.subtract)
+            st.append(st_t)
 
         z_codes = keep.tile([P, S], U32, name="z_codes", align_bytes=64)
         z_scales = keep.tile([P, S], U8, name="z_scales", align_bytes=64)
         z_all = keep.tile([P, PACK * S], BF16, name="z_all")
-        sg_early = keep.tile([P, PACK * Z_STEP], F32, name="sg_early")
-        sg_late = keep.tile([P, PACK * (S - Z_STEP)], F32, name="sg_late", tag=f"y_n1_{PACK - 1}")
-        h_ps = pair_banks("h_ps")
+        sg_first = keep.tile([P, PACK * STRETCH], F32, name="sg_first")
+        sg_later = keep.tile([P, PACK * (S - STRETCH)], F32, name="sg_later", tag=f"y_n1_{LAST}")
 
-        def h_bank(t, c0, c1):
-            return in_bank(h_ps, t, c0, c1)
+        h_low = [psum.tile([P, 2, HALF], F32, name=f"h_low{b}") for b in range(2)]
+        h_third = psum.tile([P, PACK, STRETCH], F32, name="h_third")
+        h_last = psum.tile([P, PACK - 1, STRETCH], F32, name="h_last")
+        h_last0 = psum.tile([P, STRETCH], F32, name="h_last0", tag="y_ps00")
 
-        for c0 in (0, HALF):
+        def h_acc(t, c0, c1):
+            if c0 < HALF:
+                return h_low[t // 2][:, t % 2, c0:c1]
+            if c0 < LAST_C0:
+                return h_third[:, t, :]
+            return h_last0[:] if t == 0 else h_last[:, t - 1, :]
+
+        first_in_bank = {0: (0, 2), HALF: (0,), LAST_C0: (0, 1)}
+        last_in_bank = {HALF: (1, 3), LAST_C0: (3,), S: (0, 3)}
+
+        def hashed_product(c0, c1):
             for t in range(PACK):
-                cols = slice(t * P, (t + 1) * P)
-                nc.tensor.matmul_mx(
-                    out=h_bank(t, c0, c0 + HALF),
-                    lhsT=w3_codes[:, cols].bitcast(FP8X4),
-                    lhsT_scale=w3_scales[:, cols],
-                    rhs=xh_words[:, c0 : c0 + HALF].bitcast(FP8X4),
-                    rhs_scale=xh_scales[:, c0 : c0 + HALF],
-                    start=(t < 2),
-                    stop=False,
-                )
+                start = t in first_in_bank[c0]
+                product(h_acc(t, c0, c1), w3_codes, w3_scales, t, xh_words, xh_scales, c0, c1, start, False)
 
-        for c0 in range(0, S, Z_STEP):
-            c1 = c0 + Z_STEP
-            width = c1 - c0
+        hashed_product(0, HALF)
+        hashed_product(HALF, LAST_C0)
+
+        for c0 in range(0, S, STRETCH):
+            c1 = c0 + STRETCH
             z_rows = z_all[:, PACK * c0 : PACK * c1].rearrange("p (t c) -> p t c", t=PACK)
-            z_g = keep.tile([P, width * PACK], BF16, name=f"z_g{c0}", align_bytes=64)
+            z_bf = keep.tile([P, STRETCH * PACK], BF16, name=f"z_bf{c0}", align_bytes=64)
             for t in range(PACK):
-                first = PACK * max(c0 - Z_STEP, 0) + t * width
-                sg = (sg_early if c0 == 0 else sg_late)[:, first : first + width]
+                at = PACK * max(c0 - STRETCH, 0) + t * STRETCH
+                sg = (sg_first if c0 == 0 else sg_later)[:, at : at + STRETCH]
                 nc.scalar.activation(
                     sg,
                     st[t][:].indirect(entries(n2_t, c0, c1)),
@@ -212,50 +225,60 @@ def tile_picked_mixhehqtrim_none_p_kernel(
                     scale=sl_t[:, t : t + 1],
                 )
                 nc.vector.scalar_tensor_tensor(
-                    z_rows[:, t, :], in_bank(y_ps, t, c0, c1), gn_t[:, t : t + 1], sg, ALU.mult, ALU.mult
+                    z_rows[:, t, :], y_acc(t, c0, c1), gn_t[:, t : t + 1], sg, ALU.mult, ALU.mult
                 )
             nc.vector.tensor_copy(
-                out=z_g[:].rearrange("p (c i t) -> p c t i", i=4, t=PACK),
-                in_=z_rows.rearrange("p t (c i) -> p c t i", i=4),
+                out=z_bf[:].rearrange("p (c e t) -> p c t e", e=4, t=PACK),
+                in_=z_rows.rearrange("p t (c e) -> p c t e", e=4),
             )
-            quantize(z_codes[:, c0:c1], z_scales[:, c0:c1], z_g[:])
-            for t in (3, 0, 2, 1):
-                cols = slice(t * P, (t + 1) * P)
-                nc.tensor.matmul_mx(
-                    out=h_bank(t, c0, c1),
-                    lhsT=w2_codes[:, cols].bitcast(FP8X4),
-                    lhsT_scale=w2_scales[:, cols],
-                    rhs=z_codes[:, c0:c1].bitcast(FP8X4),
-                    rhs_scale=z_scales[:, c0:c1],
-                    start=False,
-                    stop=(t < 2 and c1 % HALF == 0),
-                )
-        nc.scalar.copy(out=h_sb[0][:, HALF:S], in_=h_bank(0, HALF, S))
-        for t in range(1, PACK):
-            nc.vector.tensor_copy(out=h_sb[t][:, HALF:S], in_=h_bank(t, HALF, S))
-        for t in range(PACK):
-            nc.scalar.copy(out=h_sb[t][:, 0:HALF], in_=h_bank(t, 0, HALF))
+            quantize(z_codes[:, c0:c1], z_scales[:, c0:c1], z_bf[:])
+            if c1 == HALF:
+                hashed_product(LAST_C0, S)
+            for t in range(PACK):
+                stop = t in last_in_bank.get(c1, ())
+                product(h_acc(t, c0, c1), w2_codes, w2_scales, t, z_codes, z_scales, c0, c1, False, stop)
+
+        nc.scalar.copy(out=h_sb[0][:, LAST_C0:], in_=h_acc(0, LAST_C0, S))
+        for t in reversed(range(1, PACK)):
+            nc.vector.tensor_copy(out=h_sb[t][:, LAST_C0:], in_=h_acc(t, LAST_C0, S))
+        for c0, c1 in ((0, HALF), (HALF, LAST_C0)):
+            for t in range(PACK):
+                nc.scalar.copy(out=h_sb[t][:, c0:c1], in_=h_acc(t, c0, c1))
 
         out_rows = out.rearrange("(b t i) s -> t b i s", t=PACK, i=8)
-        steps = [(t, c0, c0 + HALF) for t in range(PACK) for c0 in (0, HALF)][:-1] + [(3, 256, 384), (3, 384, 512)]
-        rests = []
 
-        def finish(n):
-            t, c0, c1 = steps[n]
-            res = keep.tile([P, c1 - c0], F32, name=f"res_{n}")
-            nc.vector.tensor_tensor(res[:], h_sb[t][:].indirect(entries(n3_t, c0, c1)), rests[n][:], ALU.add)
-            nc.sync.dma_start(out_rows[t][:, :, c0:c1], res[:])
+        h3_end = keep.tile([P, HALF], F32, name="h3_end")
+        sum_end = keep.tile([P, HALF], F32, name="sum_end")
+        nc.vector.tensor_copy(h3_end[:], h_sb[LAST][:].indirect(entries(n3_t, HALF, S)))
+        nc.vector.tensor_tensor(sum_end[:], h3_end[:], h_sb[LAST][:, HALF:], ALU.add)
 
-        for n, (t, c0, c1) in enumerate(steps):
-            h4 = keep.tile([P, c1 - c0], F32, name=f"h4_{n}")
-            h5 = keep.tile([P, c1 - c0], F32, name=f"h5_{n}")
-            top = keep.tile([P, c1 - c0], F32, name=f"top_{n}")
-            rest = keep.tile([P, c1 - c0], F32, name=f"rest_{n}")
-            rests.append(rest)
+        def larger(t, c0, c1):
+            h4 = keep.tile([P, c1 - c0], F32, name=f"h4_{t}_{c0}")
+            h5 = keep.tile([P, c1 - c0], F32, name=f"h5_{t}_{c0}")
+            top = keep.tile([P, c1 - c0], F32, name=f"top_{t}_{c0}")
             nc.scalar.activation(h4[:], h_sb[t][:].indirect(entries(n4_t, c0, c1)), ACT.Copy)
             nc.scalar.activation(h5[:], h_sb[t][:].indirect(entries(n5_t, c0, c1)), ACT.Copy)
             nc.vector.tensor_tensor(top[:], h4[:], h5[:], ALU.max)
-            if n > 0:
-                finish(n - 1)
-            nc.vector.tensor_tensor(rest[:], h_sb[t][:, c0:c1], top[:], ALU.subtract)
-        finish(len(steps) - 1)
+            return top
+
+        def finish(t, c0, rest):
+            res = keep.tile([P, HALF], F32, name=f"res_{t}_{c0}")
+            nc.vector.tensor_tensor(res[:], h_sb[t][:].indirect(entries(n3_t, c0, c0 + HALF)), rest[:], ALU.add)
+            nc.sync.dma_start(out_rows[t][:, :, c0 : c0 + HALF], res[:])
+
+        waiting = []
+        for t, c0 in [(t, c0) for t in range(PACK) for c0 in (0, HALF)][:-1]:
+            top = larger(t, c0, c0 + HALF)
+            for step in waiting:
+                finish(*step)
+            rest = keep.tile([P, HALF], F32, name=f"rest_{t}_{c0}")
+            nc.vector.tensor_tensor(rest[:], h_sb[t][:, c0 : c0 + HALF], top[:], ALU.subtract)
+            waiting = [(t, c0, rest)]
+        for c0 in range(HALF, S, STRETCH):
+            c1 = c0 + STRETCH
+            top = larger(LAST, c0, c1)
+            if c0 == HALF:
+                finish(*waiting[0])
+            res = keep.tile([P, STRETCH], F32, name=f"res_end{c0}")
+            nc.vector.tensor_tensor(res[:], sum_end[:, c0 - HALF : c1 - HALF], top[:], ALU.subtract)
+            nc.sync.dma_start(out_rows[LAST][:, :, c0:c1], res[:])

from contextlib import ExitStack

import concourse.mybir as mybir

T, S, N, H = 2048, 512, 512, 512
FLOPS = 3 * 2 * 512 * 512 * 512

F32 = mybir.dt.float32
BF16 = mybir.dt.bfloat16
I32 = mybir.dt.int32
U32 = mybir.dt.uint32
U16 = mybir.dt.uint16
U8 = mybir.dt.uint8
FP8X4 = mybir.dt.float8_e4m3fn_x4
ALU = mybir.AluOpType
ACT = mybir.ActivationFunctionType

P = 128
PACK = 4
LAST = PACK - 1
HALF = S // 2
STRETCH = 128
LAST_C0 = S - STRETCH
PAD = 16
W1_SPLIT = 352


def tile_picked_mixhehqtrim_none_p_kernel(
    tc, x_words, x_scales, w1, sl, th, gn, w2, w3, offs, n1, n2, hz, n3, n4, n5, out
):
    nc = tc.nc
    with ExitStack() as ctx:
        keep = ctx.enter_context(tc.tile_pool(name="keep", bufs=1))
        psum = ctx.enter_context(tc.psum_pool(name="psum", bufs=1))

        def load_list(name, src):
            tile = keep.tile([P, S // 16], U16, name=name)
            nc.sync.dma_start(tile[:], src)
            return tile

        def entries(lst, c0, c1):
            return lst[:, c0 // 16 : c1 // 16]

        def load_weight(name, w, c0, c1):
            raw = keep.tile([P, PACK, c1 - c0], F32, name=name)
            nc.sync.dma_start(raw[:], w.rearrange("(p j) c -> p j c", j=PACK)[:, :, c0:c1])
            return raw

        def load_rows(name, v):
            tile = keep.tile([P, PACK], F32, name=name)
            nc.sync.dma_start(tile[:], v.rearrange("(p t) o -> p (t o)", t=PACK))
            return tile

        def quantize(codes, scales, src):
            nc.vector.quantize_mx(out=codes.bitcast(FP8X4), scales=scales, in_=src)

        def product(acc, w_codes, w_scales, t, codes, scales, c0, c1, start, stop):
            cols = slice(t * P, (t + 1) * P)
            nc.tensor.matmul_mx(
                out=acc,
                lhsT=w_codes[:, cols].bitcast(FP8X4),
                lhsT_scale=w_scales[:, cols],
                rhs=codes[:, c0:c1].bitcast(FP8X4),
                rhs_scale=scales[:, c0:c1],
                start=start,
                stop=stop,
            )

        offs_t = load_list("offs_t", offs)
        hz_t = load_list("hz_t", hz)
        w1_raw0 = load_weight("w1_raw0", w1, 0, HALF)
        xo_bytes = keep.tile([P, T], U8, name="xo_bytes", align_bytes=64)
        nc.vector.memset(xo_bytes[:].bitcast(I32), 0)
        for q in range(4):
            nc.sync.dma_start(
                xo_bytes[32 * q : 32 * q + 4, :].bitcast(I32), x_scales[0, 4 * q : 4 * q + 4, :].bitcast(I32)
            )
        xh_bytes = keep.tile([P, T], U8, name="xh_bytes", align_bytes=64)
        nc.vector.memset(xh_bytes[:].bitcast(I32), 0)
        nc.sync.dma_start(xh_bytes[0:P:8, :].bitcast(I32), x_scales[0].bitcast(I32))
        x_sb = keep.tile([P, T], I32, name="x_sb", align_bytes=64)
        nc.sync.dma_start(x_sb[:], x_words[0].rearrange("p n j -> p (n j)").bitcast(I32))
        w1_raw1 = load_weight("w1_raw1", w1, HALF, H)
        n1_t = load_list("n1_t", n1)
        sl_t = load_rows("sl_t", sl)
        th_t = load_rows("th_t", th)
        w3_raw = load_weight("w3_raw", w3, 0, N)
        w2_raw = load_weight("w2_raw", w2, 0, N)
        n2_t = load_list("n2_t", n2)
        gn_t = load_rows("gn_t", gn)
        n4_t = load_list("n4_t", n4)
        n5_t = load_list("n5_t", n5)
        n3_t = load_list("n3_t", n3)

        warm_in = keep.tile([P, 8], F32, name="warm_in")
        warm_out = keep.tile([P, 8], F32, name="warm_out")
        nc.vector.memset(warm_in[:], 0.0)
        nc.scalar.activation(warm_out[:], warm_in[:], ACT.Sigmoid)

        xo_scales = keep.tile([P, S], U8, name="xo_scales", align_bytes=64)
        xo_words = keep.tile([P, S], U32, name="xo_words", align_bytes=64)
        nc.vector.tensor_copy(xo_scales[:], xo_bytes[:].indirect(offs_t[:]))
        nc.vector.tensor_copy(xo_words[:], x_sb[:].bitcast(U32).indirect(offs_t[:]))

        w1_bf = keep.tile([P, PACK * H], BF16, name="w1_bf", tag="w1_stage", align_bytes=64)
        w1_codes = keep.tile([P, H], U32, name="w1_codes", align_bytes=64)
        w1_scales = keep.tile([P, H], U8, name="w1_scales", align_bytes=64)

        def round_w1(copy, raw, raw_c0, c0, c1):
            copy(
                out=w1_bf[:].rearrange("p (t m j) -> p m t j", t=PACK, j=PACK)[:, c0 // PACK : c1 // PACK],
                in_=raw[:, :, c0 - raw_c0 : c1 - raw_c0].rearrange("p j (m t) -> p m t j", t=PACK),
            )

        round_w1(nc.scalar.copy, w1_raw0, 0, 0, HALF)
        round_w1(nc.scalar.copy, w1_raw1, HALF, HALF, W1_SPLIT)
        round_w1(nc.vector.tensor_copy, w1_raw1, HALF, W1_SPLIT, H)

        y_ps = [
            [psum.tile([P, 2, HALF], F32, name=f"y_ps{u}{b}", tag=f"y_ps{u}{b}") for b in range(2)] for u in range(2)
        ]

        def y_acc(t, c0, c1):
            u = c0 // HALF
            return y_ps[u][(t + 1) // 2 % 2][:, t // 2, c0 - u * HALF : c1 - u * HALF]

        y_sb = [keep.tile([P, S + PAD], F32, name=f"y_sb{t}") for t in range(PACK)]
        for t in range(PACK):
            nc.vector.memset(y_sb[t][:, S:], 0.0)
        for t in range(PACK):
            cols = slice(t * P, (t + 1) * P)
            quantize(w1_codes[:, cols], w1_scales[:, cols], w1_bf[:, t * H : (t + 1) * H])
        for t in range(PACK):
            copy = nc.vector.tensor_copy if t == LAST else nc.scalar.copy
            for c0 in (0, HALF):
                c1 = c0 + HALF
                product(y_acc(t, c0, c1), w1_codes, w1_scales, t, xo_words, xo_scales, c0, c1, True, True)
                copy(out=y_sb[t][:, c0:c1], in_=y_acc(t, c0, c1))

        xh_picked = keep.tile([P, S], U8, name="xh_picked", align_bytes=64)
        xh_words = keep.tile([P, S], U32, name="xh_words", tag="w1_stage", align_bytes=64)
        xh_scales = keep.tile([P, S], U8, name="xh_scales", align_bytes=64)
        nc.vector.tensor_copy(xh_picked[:], xh_bytes[:].indirect(hz_t[:]))
        nc.vector.tensor_copy(xh_scales[:].bitcast(I32), xh_picked[:].bitcast(I32))
        nc.vector.tensor_copy(xh_words[:], x_sb[:].bitcast(U32).indirect(hz_t[:]))
        for r in (1, 2, 3):
            nc.sync.dma_start(xh_scales[r:P:32, :].bitcast(I32), xh_picked[8 * r : P : 32, :].bitcast(I32))

        bias_t = keep.tile([P, PACK], F32, name="bias_t")
        nc.vector.scalar_tensor_tensor(bias_t[:], th_t[:], -1.0, sl_t[:], ALU.mult, ALU.mult)

        h_sb = [keep.tile([P, S], F32, name=f"h_sb{t}") for t in range(PACK)]
        y_n1 = [keep.tile([P, S], F32, name=f"y_n1_{t}", tag=f"y_n1_{t}") for t in range(PACK)]
        for t in range(PACK):
            nc.scalar.activation(y_n1[t][:], y_sb[t][:].indirect(n1_t[:]), ACT.Copy)

        def quantize_weight(name, raw):
            codes = keep.tile([P, N], U32, name=f"{name}_codes", align_bytes=64)
            scales = keep.tile([P, N], U8, name=f"{name}_scales", align_bytes=64)
            rounded = []
            for t in range(PACK):
                bf = keep.tile([P, PACK * P], BF16, name=f"{name}_bf{t}", tag=f"{name}_stage{t}", align_bytes=64)
                nc.vector.tensor_copy(
                    out=bf[:].rearrange("p (b q e j) -> p b q j e", q=2, e=4, j=PACK),
                    in_=raw[:].rearrange("p j (b t q e) -> p t b q j e", t=PACK, q=2, e=4)[:, t],
                )
                rounded.append(bf)
            for t in range(PACK):
                cols = slice(t * P, (t + 1) * P)
                quantize(codes[:, cols], scales[:, cols], rounded[t][:])
            return codes, scales

        w3_codes, w3_scales = quantize_weight("w3", w3_raw)
        w2_codes, w2_scales = quantize_weight("w2", w2_raw)

        st = []
        for t in range(PACK):
            st_t = keep.tile([P, S], F32, name=f"st{t}", tag=f"w2_stage{t}", align_bytes=64)
            for c0 in (0, HALF):
                c1 = c0 + HALF
                nc.vector.tensor_tensor(st_t[:, c0:c1], y_acc(t, c0, c1), y_n1[t][:, c0:c1], ALU.subtract)
            st.append(st_t)

        z_codes = keep.tile([P, S], U32, name="z_codes", align_bytes=64)
        z_scales = keep.tile([P, S], U8, name="z_scales", align_bytes=64)
        z_all = keep.tile([P, PACK * S], BF16, name="z_all")
        sg_first = keep.tile([P, PACK * STRETCH], F32, name="sg_first")
        sg_later = keep.tile([P, PACK * (S - STRETCH)], F32, name="sg_later", tag=f"y_n1_{LAST}")

        h_low = [psum.tile([P, 2, HALF], F32, name=f"h_low{b}") for b in range(2)]
        h_third = psum.tile([P, PACK, STRETCH], F32, name="h_third")
        h_last = psum.tile([P, PACK - 1, STRETCH], F32, name="h_last")
        h_last0 = psum.tile([P, STRETCH], F32, name="h_last0", tag="y_ps00")

        def h_acc(t, c0, c1):
            if c0 < HALF:
                return h_low[t // 2][:, t % 2, c0:c1]
            if c0 < LAST_C0:
                return h_third[:, t, :]
            return h_last0[:] if t == 0 else h_last[:, t - 1, :]

        first_in_bank = {0: (0, 2), HALF: (0,), LAST_C0: (0, 1)}
        last_in_bank = {HALF: (1, 3), LAST_C0: (3,), S: (0, 3)}

        def hashed_product(c0, c1):
            for t in range(PACK):
                start = t in first_in_bank[c0]
                product(h_acc(t, c0, c1), w3_codes, w3_scales, t, xh_words, xh_scales, c0, c1, start, False)

        hashed_product(0, HALF)
        hashed_product(HALF, LAST_C0)

        for c0 in range(0, S, STRETCH):
            c1 = c0 + STRETCH
            z_rows = z_all[:, PACK * c0 : PACK * c1].rearrange("p (t c) -> p t c", t=PACK)
            z_bf = keep.tile([P, STRETCH * PACK], BF16, name=f"z_bf{c0}", align_bytes=64)
            for t in range(PACK):
                at = PACK * max(c0 - STRETCH, 0) + t * STRETCH
                sg = (sg_first if c0 == 0 else sg_later)[:, at : at + STRETCH]
                nc.scalar.activation(
                    sg,
                    st[t][:].indirect(entries(n2_t, c0, c1)),
                    ACT.Sigmoid,
                    bias=bias_t[:, t : t + 1],
                    scale=sl_t[:, t : t + 1],
                )
                nc.vector.scalar_tensor_tensor(
                    z_rows[:, t, :], y_acc(t, c0, c1), gn_t[:, t : t + 1], sg, ALU.mult, ALU.mult
                )
            nc.vector.tensor_copy(
                out=z_bf[:].rearrange("p (c e t) -> p c t e", e=4, t=PACK),
                in_=z_rows.rearrange("p t (c e) -> p c t e", e=4),
            )
            quantize(z_codes[:, c0:c1], z_scales[:, c0:c1], z_bf[:])
            if c1 == HALF:
                hashed_product(LAST_C0, S)
            for t in range(PACK):
                stop = t in last_in_bank.get(c1, ())
                product(h_acc(t, c0, c1), w2_codes, w2_scales, t, z_codes, z_scales, c0, c1, False, stop)

        nc.scalar.copy(out=h_sb[0][:, LAST_C0:], in_=h_acc(0, LAST_C0, S))
        for t in reversed(range(1, PACK)):
            nc.vector.tensor_copy(out=h_sb[t][:, LAST_C0:], in_=h_acc(t, LAST_C0, S))
        for c0, c1 in ((0, HALF), (HALF, LAST_C0)):
            for t in range(PACK):
                nc.scalar.copy(out=h_sb[t][:, c0:c1], in_=h_acc(t, c0, c1))

        out_rows = out.rearrange("(b t i) s -> t b i s", t=PACK, i=8)

        h3_end = keep.tile([P, HALF], F32, name="h3_end")
        sum_end = keep.tile([P, HALF], F32, name="sum_end")
        nc.vector.tensor_copy(h3_end[:], h_sb[LAST][:].indirect(entries(n3_t, HALF, S)))
        nc.vector.tensor_tensor(sum_end[:], h3_end[:], h_sb[LAST][:, HALF:], ALU.add)

        def larger(t, c0, c1):
            h4 = keep.tile([P, c1 - c0], F32, name=f"h4_{t}_{c0}")
            h5 = keep.tile([P, c1 - c0], F32, name=f"h5_{t}_{c0}")
            top = keep.tile([P, c1 - c0], F32, name=f"top_{t}_{c0}")
            nc.scalar.activation(h4[:], h_sb[t][:].indirect(entries(n4_t, c0, c1)), ACT.Copy)
            nc.scalar.activation(h5[:], h_sb[t][:].indirect(entries(n5_t, c0, c1)), ACT.Copy)
            nc.vector.tensor_tensor(top[:], h4[:], h5[:], ALU.max)
            return top

        def finish(t, c0, rest):
            res = keep.tile([P, HALF], F32, name=f"res_{t}_{c0}")
            nc.vector.tensor_tensor(res[:], h_sb[t][:].indirect(entries(n3_t, c0, c0 + HALF)), rest[:], ALU.add)
            nc.sync.dma_start(out_rows[t][:, :, c0 : c0 + HALF], res[:])

        waiting = []
        for t, c0 in [(t, c0) for t in range(PACK) for c0 in (0, HALF)][:-1]:
            top = larger(t, c0, c0 + HALF)
            for step in waiting:
                finish(*step)
            rest = keep.tile([P, HALF], F32, name=f"rest_{t}_{c0}")
            nc.vector.tensor_tensor(rest[:], h_sb[t][:, c0 : c0 + HALF], top[:], ALU.subtract)
            waiting = [(t, c0, rest)]
        for c0 in range(HALF, S, STRETCH):
            c1 = c0 + STRETCH
            top = larger(LAST, c0, c1)
            if c0 == HALF:
                finish(*waiting[0])
            res = keep.tile([P, STRETCH], F32, name=f"res_end{c0}")
            nc.vector.tensor_tensor(res[:], sum_end[:, c0 - HALF : c1 - HALF], top[:], ALU.subtract)
            nc.sync.dma_start(out_rows[LAST][:, :, c0:c1], res[:])
